import numpy as np
import ml_dtypes


def mxq(x, axis, fmt="e4m3"):
    dtype, down = {"e4m3": (ml_dtypes.float8_e4m3fn, 7), "e5m2": (ml_dtypes.float8_e5m2, 14)}[fmt]
    v = np.moveaxis(np.asarray(x, np.float32).astype(ml_dtypes.bfloat16).astype(np.float64), axis, -1)
    blocks = v.reshape(v.shape[:-1] + (-1, 32))
    amax = np.abs(blocks).max(-1, keepdims=True)
    byte = np.maximum(np.where(amax > 0, np.frexp(amax)[1] - 1 + 127, 0) - down, 1)
    scale = np.exp2(byte - 127.0)
    codes = (blocks / scale).astype(np.float32).astype(dtype).astype(np.float64)
    return np.moveaxis((codes * scale).reshape(v.shape), -1, axis)


WIDE = False


def mx_kscale(k):
    if not WIDE:
        return np.ones(k)
    levels = np.array([10, -10, 5, -5, 0])
    if k % 512:
        return np.exp2(np.random.permutation(np.resize(levels, k // 32))).repeat(32)
    a = np.empty((k // 512, 16))
    for p in range(k // 512):
        a[p, :8] = np.random.permutation(np.resize(levels, 8))
        for g in range(8):
            far = levels[np.abs(levels - a[p, g]) >= 10]
            a[p, g + 8] = far[np.random.randint(len(far))]
    return np.exp2(a.ravel()).repeat(32)


def f64(x):
    return np.asarray(x).astype(np.float64)


def striped(idx):
    return np.tile(idx.reshape(-1, 16).T, (8, 1)).astype(np.uint16)


def unstriped(offs):
    return offs[:16].T.reshape(-1).astype(np.int64)


def pack_weight(w):
    k, n = w.shape
    w = f64(np.asarray(w, np.float32).astype(ml_dtypes.bfloat16)).reshape(k // 32, 32, n)
    amax = np.abs(w).max(1)
    byte = np.clip(np.where(amax > 0, np.frexp(amax)[1] - 1 + 127 - 7, 1), 1, 254)
    scaled = (w * np.exp2(127.0 - byte)[:, None, :]).reshape(k, n).astype(np.float32)
    words = np.ascontiguousarray(scaled.reshape(k // 512, 128, 4, n).transpose(0, 1, 3, 2)).astype(ml_dtypes.float8_e4m3fn).view(np.uint8)
    return words, np.ascontiguousarray(byte.astype(np.uint8).reshape(k // 512, 16, n))


def unpack_weight(words, scales):
    g, p, n, _ = words.shape
    vals = np.ascontiguousarray(words).view(ml_dtypes.float8_e4m3fn).astype(np.float64) * np.repeat(np.exp2(scales.astype(np.float64) - 127.0), 8, axis=1)[..., None]
    return vals.transpose(0, 1, 3, 2).reshape(g * 512, n)


E2M1 = np.array([0.0, 0.5, 1.0, 1.5, 2.0, 3.0, 4.0, 6.0, -0.0, -0.5, -1.0, -1.5, -2.0, -3.0, -4.0, -6.0])


def pack_fp4(w):
    k, n = w.shape
    w = f64(np.asarray(w, np.float32).astype(ml_dtypes.bfloat16)).reshape(k // 32, 32, n)
    amax = np.abs(w).max(1)
    mant, ex = np.frexp(amax / 6.0)
    byte = np.clip(np.where(amax > 0, np.where(mant > 0.5, ex, ex - 1) + 127, 1), 1, 254)
    scaled = (w * np.exp2(127.0 - byte)[:, None, :]).reshape(k, n).astype(np.float32)
    c = np.ascontiguousarray(scaled.reshape(k // 512, 128, 4, n).transpose(0, 1, 3, 2)).astype(ml_dtypes.float4_e2m1fn).view(np.uint8) & 0xF
    words = (c[..., 0::2] | (c[..., 1::2] << 4)).reshape(k // 512, 128, 2 * n)
    return np.ascontiguousarray(words), np.ascontiguousarray(byte.astype(np.uint8).reshape(k // 512, 16, n))


def unpack_fp4(words, scales):
    g, _, n = scales.shape
    words = np.ascontiguousarray(words).reshape(g, 128, n, 2)
    nib = np.empty((g, 128, n, 4), np.uint8)
    nib[..., 0::2] = words & 0xF
    nib[..., 1::2] = words >> 4
    vals = E2M1[nib] * np.repeat(np.exp2(scales.astype(np.float64) - 127.0), 8, axis=1)[..., None]
    return vals.transpose(0, 1, 3, 2).reshape(g * 512, n)


def planes(y):
    n, m = y.shape
    v = y.astype(np.float32).astype(ml_dtypes.bfloat16).astype(np.float64).reshape(n // 32, 32, m)
    top = np.abs(v).max(1)
    byte = np.clip(np.where(top > 0, np.frexp(top)[1] - 1 + 127 - 7, 1), 1, 254)
    codes = (v * np.exp2(127.0 - byte)[:, None, :]).reshape(n, m).astype(np.float32).astype(ml_dtypes.float8_e4m3fn).view(np.uint8)
    words = codes.reshape(n // 512, 128, 4, m).transpose(0, 1, 3, 2)
    return np.ascontiguousarray(words), np.ascontiguousarray(byte.astype(np.uint8).reshape(n // 512, 16, m))


K, T, S, H, Z, W = 512, 2048, 512, 512, 512, 2048


def setup_inputs():
    n = np.random.standard_normal
    s = mx_kscale(K)[:, None]
    u = mx_kscale(H)
    packed_xT = pack_weight(n((K, T)) * s)
    packed_w1 = pack_fp4(n((K, H)) / np.sqrt(K) / s)
    packed_eT = pack_weight(n((K, W)) * s)
    packed_w2 = pack_fp4(n((K, H)) / np.sqrt(K) / s)
    packed_w3 = pack_fp4(n((K, H)) / np.sqrt(K) / s)
    return {
        "x_words": packed_xT[0],
        "x_scales": packed_xT[1],
        "w1_words": packed_w1[0],
        "w1_scales": packed_w1[1],
        "e_words": packed_eT[0],
        "e_scales": packed_eT[1],
        "w2_words": packed_w2[0],
        "w2_scales": packed_w2[1],
        "w3_words": packed_w3[0],
        "w3_scales": packed_w3[1],
        "unit": (np.random.uniform(0.6, 1.4, (H, 1)) * u[:, None]).astype(np.float32),
        "unit2": (np.random.uniform(0.6, 1.4, (H, 1)) / np.sqrt(H) / u[:, None]).astype(np.float32),
        "offs": striped(np.random.permutation(T)[:S]),
        "gal": striped(np.random.permutation(W)[:Z]),
        "cam": striped(np.random.permutation(Z)),
        "nn1": striped(np.random.permutation(Z)),
        "nn2": striped(np.random.permutation(Z)),
    }


def reference(x_words, x_scales, w1_words, w1_scales, e_words, e_scales, w2_words, w2_scales, w3_words, w3_scales, unit, unit2, offs, gal, cam, nn1, nn2):
    xq = unpack_weight(x_words, x_scales)[:, unstriped(offs)]
    y = unpack_fp4(w1_words, w1_scales).T @ xq
    pb = np.tanh(y)
    hid = f64(unit) * pb
    e_gal = unpack_weight(e_words, e_scales)[:, unstriped(gal)]
    ye = unpack_fp4(w2_words, w2_scales).T @ e_gal
    yg = unpack_fp4(w3_words, w3_scales).T @ e_gal
    gc = yg[:, unstriped(cam)]
    aug = ye + 0.5 * gc
    hid2 = f64(unit2) * aug
    sc = mxq(hid, 0, "e4m3").T @ mxq(hid2, 0, "e4m3")
    s1 = sc[:, unstriped(nn1)]
    s2 = sc[:, unstriped(nn2)]
    ngb = s1 + s2
    out_0 = sc * ngb - (0.3 * sc)
    return (out_0,) + planes(out_0)

@@ -1,0 +1,258 @@
+from contextlib import ExitStack
+
+import concourse.mybir as mybir
+from concourse.masks import make_identity
+
+K, T, S, H = 512, 2048, 512, 512
+FLOPS = 4 * 2 * K * S * H
+
+F32 = mybir.dt.float32
+BF16 = mybir.dt.bfloat16
+I32 = mybir.dt.int32
+U32 = mybir.dt.uint32
+U16 = mybir.dt.uint16
+U8 = mybir.dt.uint8
+FP8X4 = mybir.dt.float8_e4m3fn_x4
+FP4X4 = mybir.dt.float4_e2m1fn_x4
+ACT = mybir.ActivationFunctionType
+ALU = mybir.AluOpType
+
+P = 128
+PACK = 4
+HALF = S // 2
+LIST_COLS = S // 16
+
+
+def tile_picked_yreidr_mul_po_kernel(
+    tc, x_words, x_scales, w1_words, w1_scales, e_words, e_scales, w2_words, w2_scales, w3_words, w3_scales,
+    unit, unit2, offs, gal, cam, nn1, nn2, out_0, out_1, out_2,
+):
+    nc = tc.nc
+    with ExitStack() as ctx:
+        keep = ctx.enter_context(tc.tile_pool(name="keep", bufs=1))
+        psum = ctx.enter_context(tc.psum_pool(name="psum", bufs=1))
+
+        def sb(name, shape, dtype):
+            return keep.tile(shape, dtype, name=name, align_bytes=64)
+
+        def bank(b, shape):
+            return psum.tile(shape, F32, name="bank%d" % b, tag="bank%d" % b)
+
+        def load_list(name, src):
+            t = keep.tile([P, LIST_COLS], U16, name=name)
+            nc.sync.dma_start(t[:], src)
+            return t
+
+        def zeroed_plane(name, width, engine):
+            t = sb(name, [P, width], U8)
+            engine.memset(t[:].bitcast(I32), 0)
+            return t
+
+        def load_scale_rows(t, src, q, queue):
+            queue.dma_start(t[32 * q : 32 * q + 4, :].bitcast(I32), src[0, 4 * q : 4 * q + 4, :].bitcast(I32))
+
+        def load_table(name, src):
+            t = sb(name, [P, T], I32)
+            nc.sync.dma_start(t[:], src[0].rearrange("p n t -> p (n t)").bitcast(I32))
+            return t
+
+        def load_weight(name, src, queue):
+            t = sb(name, [P, 2 * H], U8)
+            queue.dma_start(t[:].bitcast(I32), src[0].bitcast(I32))
+            return t
+
+        def deal(name, raw, width):
+            t = sb(name, [P, width], U8)
+            nc.vector.tensor_copy(
+                t[:].bitcast(I32).rearrange("p (s b q) -> p s b q", s=PACK, b=16),
+                raw.bitcast(I32).rearrange("p (b s q) -> p s b q", s=PACK, b=16),
+            )
+            return t
+
+        def half_list(lst, h):
+            return lst[:, h * (LIST_COLS // 2) : (h + 1) * (LIST_COLS // 2)]
+
+        def cols(h):
+            return slice(h * HALF, (h + 1) * HALF)
+
+        es_win = zeroed_plane("es_win", T, nc.vector)
+        unit_rows = sb("unit_rows", [P, P], F32)
+        nc.gpsimd.memset(unit_rows[:], 0.0)
+        ws_raw = zeroed_plane("ws_raw", 3 * H, nc.vector)
+        w1s_raw, w2s_raw, w3s_raw = [ws_raw[:, i * H : (i + 1) * H] for i in range(3)]
+        xs_win = zeroed_plane("xs_win", T, nc.vector)
+
+        nc.gpsimd.dma_start(
+            unit_rows[PACK : 2 * PACK, :].rearrange("s (b r) -> s b r", r=8),
+            unit2.rearrange("(b s r) o -> s b (r o)", s=PACK, r=8),
+        )
+        nc.gpsimd.dma_start(
+            unit_rows[0:PACK, :].rearrange("s (b r) -> s b r", r=8),
+            unit.rearrange("(b s r) o -> s b (r o)", s=PACK, r=8),
+        )
+        ident = sb("ident", [P, P], F32)
+        make_identity(nc, ident[:])
+
+        gal_t = load_list("gal_t", gal)
+        w3_raw = load_weight("w3_raw", w3_words, nc.scalar)
+        ew_win = load_table("ew_win", e_words)
+        for q in range(4):
+            load_scale_rows(es_win, e_scales, q, nc.sync if q % 2 else nc.scalar)
+        for q in range(4):
+            load_scale_rows(w3s_raw, w3_scales, q, nc.scalar)
+        offs_t = load_list("offs_t", offs)
+        for q in range(4):
+            load_scale_rows(xs_win, x_scales, q, nc.scalar if q == 3 else nc.sync)
+        cam_t = load_list("cam_t", cam)
+        w2_raw = load_weight("w2_raw", w2_words, nc.sync)
+        for q in range(4):
+            load_scale_rows(w2s_raw, w2_scales, q, nc.sync)
+        xw_win = load_table("xw_win", x_words)
+        w1_raw = load_weight("w1_raw", w1_words, nc.sync)
+        for q in range(4):
+            load_scale_rows(w1s_raw, w1_scales, q, nc.sync)
+        nn1_t = load_list("nn1_t", nn1)
+        nn2_t = load_list("nn2_t", nn2)
+
+        es = sb("es", [P, S], U8)
+        nc.vector.tensor_copy(es[:], es_win[:].indirect(gal_t[:]))
+        ew = sb("ew", [P, S], U32)
+        nc.vector.tensor_copy(ew[:], ew_win[:].bitcast(U32).indirect(gal_t[:]))
+        w3 = deal("w3", w3_raw[:], 2 * H)
+        w3s = deal("w3s", w3s_raw, H)
+
+        unit_ps = bank(4, [P, P])
+        nc.tensor.transpose(unit_ps[:], unit_rows[:], ident[:])
+        units = sb("units", [P, 2 * PACK], F32)
+        nc.scalar.copy(units[:], unit_ps[:, 0 : 2 * PACK])
+        unit2_half = sb("unit2_half", [P, PACK], F32)
+        nc.scalar.activation(unit2_half[:], unit_ps[:, PACK : 2 * PACK], ACT.Copy, scale=0.5)
+
+        def weight_mm(out, w, ws, s, rhs, rhs_scale):
+            nc.tensor.matmul_mx(
+                out=out,
+                lhsT=w[:, s * 2 * P : (s + 1) * 2 * P].bitcast(FP4X4),
+                lhsT_scale=ws[:, s * P : (s + 1) * P],
+                rhs=rhs.bitcast(FP8X4),
+                rhs_scale=rhs_scale,
+                start=True,
+                stop=True,
+            )
+
+        yg_ps = []
+        for s in range(PACK):
+            b = bank(s, [P, S])
+            weight_mm(b[:], w3, w3s, s, ew[:], es[:])
+            yg_ps.append(b)
+
+        xs = sb("xs", [P, S], U8)
+        nc.vector.tensor_copy(xs[:], xs_win[:].indirect(offs_t[:]))
+
+        gcs = []
+        for s in range(PACK):
+            win = sb("yg_win%d" % s, [P, S], F32)
+            gc = sb("gc%d" % s, [P, S], F32)
+            if s == 1:
+                nc.vector.tensor_scalar(win[:], yg_ps[s][:], unit2_half[:, s : s + 1], None, ALU.mult)
+                for h in range(2):
+                    nc.vector.tensor_copy(gc[:, cols(h)], win[:].indirect(half_list(cam_t, h)))
+            else:
+                nc.scalar.activation(win[:], yg_ps[s][:], ACT.Copy, scale=unit2_half[:, s : s + 1])
+                for h in range(2):
+                    nc.scalar.activation(gc[:, cols(h)], win[:].indirect(half_list(cam_t, h)), ACT.Copy)
+            gcs.append(gc)
+
+        w2 = deal("w2", w2_raw[:], 2 * H)
+        w2s = deal("w2s", w2s_raw, H)
+        ye_ps = []
+        for s in range(PACK):
+            b = bank(4 + s, [P, S])
+            weight_mm(b[:], w2, w2s, s, ew[:], es[:])
+            ye_ps.append(b)
+
+        hid2_rows = sb("hid2_rows", [P, PACK, S], BF16)
+
+        def combine(s):
+            nc.vector.scalar_tensor_tensor(
+                hid2_rows[:, s, :], ye_ps[s][:], units[:, PACK + s : PACK + s + 1], gcs[s][:], ALU.mult, ALU.add
+            )
+
+        combine(0)
+        combine(1)
+        xw = sb("xw", [P, S], U32)
+        nc.vector.tensor_copy(xw[:], xw_win[:].bitcast(U32).indirect(offs_t[:]))
+        w1 = deal("w1", w1_raw[:], 2 * H)
+        w1s = deal("w1s", w1s_raw, H)
+        combine(2)
+        combine(3)
+
+        pb = sb("pb", [P, PACK, P, PACK], F32)
+        for c in range(4):
+            b = bank(c, [P, PACK, P])
+            for s in range(PACK):
+                weight_mm(b[:, s, :], w1, w1s, s, xw[:, c * P : (c + 1) * P], xs[:, c * P : (c + 1) * P])
+            nc.scalar.activation(
+                pb[:, :, 32 * c : 32 * (c + 1), :], b[:].rearrange("p s (m j) -> p j m s", j=PACK), ACT.Tanh
+            )
+
+        hid2_in = sb("hid2_in", [P, S, PACK], BF16)
+        nc.vector.tensor_copy(
+            hid2_in[:].rearrange("p (c i) s -> p c s i", i=4), hid2_rows[:].rearrange("p s (c i) -> p c s i", i=4)
+        )
+        hid2_codes = sb("hid2_codes", [P, S], U32)
+        hid2_scales = sb("hid2_scales", [P, S], U8)
+        nc.vector.quantize_mx(
+            out=hid2_codes[:].bitcast(FP8X4), scales=hid2_scales[:], in_=hid2_in[:].rearrange("p c s -> p (c s)")
+        )
+
+        sc_ps = []
+        for j in range(PACK):
+            hid_in = sb("hid_in%d" % j, [P, P, PACK], BF16)
+            nc.vector.tensor_tensor(
+                hid_in[:], pb[:, j, :, :], units[:, 0:PACK].unsqueeze(1).to_broadcast([P, P, PACK]), ALU.mult
+            )
+            hid_codes = sb("hid_codes%d" % j, [P, P], U32)
+            hid_scales = sb("hid_scales%d" % j, [P, P], U8)
+            nc.vector.quantize_mx(
+                out=hid_codes[:].bitcast(FP8X4), scales=hid_scales[:], in_=hid_in[:].rearrange("p c s -> p (c s)")
+            )
+            b = bank(4 + j, [P, S])
+            nc.tensor.matmul_mx(
+                out=b[:], lhsT=hid_codes[:].bitcast(FP8X4), lhsT_scale=hid_scales[:],
+                rhs=hid2_codes[:].bitcast(FP8X4), rhs_scale=hid2_scales[:], start=True, stop=True,
+            )
+            sc_ps.append(b)
+
+        out_rows = out_0.rearrange("(p j) e -> p j e", j=PACK)
+        words_out = out_1[0].rearrange("p n t -> p (n t)").bitcast(I32)
+        out_codes = sb("out_codes", [P, S], I32)
+        out_scales = sb("out_scales", [P, S], U8)
+        sc_win = []
+        for h in range(2):
+            res = sb("res%d" % h, [P, PACK, HALF], F32)
+            for j in range(PACK):
+                if h == 0:
+                    win = sb("sc_win%d" % j, [P, S], F32)
+                    nc.scalar.activation(win[:], sc_ps[j][:], ACT.Copy, bias=-0.15)
+                    sc_win.append(win)
+                s1 = sb("s1_%d_%d" % (h, j), [P, HALF], F32)
+                nc.scalar.activation(s1[:], sc_win[j][:].indirect(half_list(nn1_t, h)), ACT.Copy)
+                ngb = sb("ngb_%d_%d" % (h, j), [P, HALF], F32)
+                nc.vector.tensor_tensor(ngb[:], sc_win[j][:].indirect(half_list(nn2_t, h)), s1[:], ALU.add)
+                nc.vector.tensor_tensor(res[:, j, :], sc_ps[j][:, cols(h)], ngb[:], ALU.mult)
+            nc.sync.dma_start(out_rows[:, :, cols(h)], res[:])
+            res_in = sb("res_in%d" % h, [P, HALF, PACK], BF16)
+            src = res[:].rearrange("p s (c i) -> p c s i", i=4)
+            dst = res_in[:].rearrange("p (c i) s -> p c s i", i=4)
+            if h == 0:
+                nc.scalar.copy(dst, src)
+            else:
+                nc.vector.tensor_copy(dst, src)
+            nc.vector.quantize_mx(
+                out=out_codes[:, cols(h)].bitcast(FP8X4), scales=out_scales[:, cols(h)],
+                in_=res_in[:].rearrange("p c s -> p (c s)"),
+            )
+            nc.sync.dma_start(words_out[:, cols(h)], out_codes[:, cols(h)])
+        for q in range(4):
+            queue = nc.sync if q < 2 else nc.scalar
+            queue.dma_start(out_2[0, 4 * q : 4 * q + 4, :].bitcast(I32), out_scales[32 * q : 32 * q + 4, :].bitcast(I32))

@@ -1,7 +1,6 @@
 from contextlib import ExitStack
 
 import concourse.mybir as mybir
-from concourse.masks import make_identity
 
 K, T, S, H = 512, 2048, 512, 512
 FLOPS = 4 * 2 * K * S * H
@@ -21,6 +20,11 @@ P = 128
 PACK = 4
 HALF = S // 2
 LIST_COLS = S // 16
+ON_VECTOR = [(1, 0), (1, 1)]
+SPLIT = 256
+ILB = 1
+EV = []
+STEPS = [(0,0),(1,0),(0,1),(1,1),(0,2),(0,3),(1,2),(1,3)]
 
 
 def tile_picked_yreidr_mul_po_kernel(
@@ -32,8 +36,8 @@ def tile_picked_yreidr_mul_po_kernel(
         keep = ctx.enter_context(tc.tile_pool(name="keep", bufs=1))
         psum = ctx.enter_context(tc.psum_pool(name="psum", bufs=1))
 
-        def sb(name, shape, dtype):
-            return keep.tile(shape, dtype, name=name, align_bytes=64)
+        def sb(name, shape, dtype, tag=None):
+            return keep.tile(shape, dtype, name=name, tag=tag or name, align_bytes=64)
 
         def bank(b, shape):
             return psum.tile(shape, F32, name="bank%d" % b, tag="bank%d" % b)
@@ -51,9 +55,9 @@ def tile_picked_yreidr_mul_po_kernel(
         def load_scale_rows(t, src, q, queue):
             queue.dma_start(t[32 * q : 32 * q + 4, :].bitcast(I32), src[0, 4 * q : 4 * q + 4, :].bitcast(I32))
 
-        def load_table(name, src):
+        def load_table(name, src, queue):
             t = sb(name, [P, T], I32)
-            nc.sync.dma_start(t[:], src[0].rearrange("p n t -> p (n t)").bitcast(I32))
+            queue.dma_start(t[:], src[0].rearrange("p n t -> p (n t)").bitcast(I32))
             return t
 
         def load_weight(name, src, queue):
@@ -61,8 +65,8 @@ def tile_picked_yreidr_mul_po_kernel(
             queue.dma_start(t[:].bitcast(I32), src[0].bitcast(I32))
             return t
 
-        def deal(name, raw, width):
-            t = sb(name, [P, width], U8)
+        def deal(name, raw, width, tag=None):
+            t = sb(name, [P, width], U8, tag=tag)
             nc.vector.tensor_copy(
                 t[:].bitcast(I32).rearrange("p (s b q) -> p s b q", s=PACK, b=16),
                 raw.bitcast(I32).rearrange("p (b s q) -> p s b q", s=PACK, b=16),
@@ -76,38 +80,42 @@ def tile_picked_yreidr_mul_po_kernel(
             return slice(h * HALF, (h + 1) * HALF)
 
         es_win = zeroed_plane("es_win", T, nc.vector)
-        unit_rows = sb("unit_rows", [P, P], F32)
+        unit_rows = sb("unit_rows", [P, 2 * P], F32)
         nc.gpsimd.memset(unit_rows[:], 0.0)
-        ws_raw = zeroed_plane("ws_raw", 3 * H, nc.vector)
-        w1s_raw, w2s_raw, w3s_raw = [ws_raw[:, i * H : (i + 1) * H] for i in range(3)]
+        ws_raw = zeroed_plane("ws_raw", 2 * H, nc.vector)
         xs_win = zeroed_plane("xs_win", T, nc.vector)
-
-        nc.gpsimd.dma_start(
-            unit_rows[PACK : 2 * PACK, :].rearrange("s (b r) -> s b r", r=8),
-            unit2.rearrange("(b s r) o -> s b (r o)", s=PACK, r=8),
-        )
-        nc.gpsimd.dma_start(
-            unit_rows[0:PACK, :].rearrange("s (b r) -> s b r", r=8),
-            unit.rearrange("(b s r) o -> s b (r o)", s=PACK, r=8),
-        )
+        w1s_raw = zeroed_plane("w1s_raw", H, nc.vector)
+        zeros = sb("zeros", [P, P], F32, tag="xw_win")
+        nc.gpsimd.memset(zeros[:], 0.0)
         ident = sb("ident", [P, P], F32)
-        make_identity(nc, ident[:])
+        nc.gpsimd.affine_select(
+            out=ident[:], in_=zeros[:], compare_op=ALU.not_equal, fill=1.0, base=0, pattern=[[-1, P]], channel_multiplier=1
+        )
 
+        def load_unit(col, src):
+            nc.sync.dma_start(
+                unit_rows[0:PACK, col : col + P].rearrange("s (b r) -> s b r", r=8),
+                src.rearrange("(b s r) o -> s b (r o)", s=PACK, r=8),
+            )
+
+        ws_rows = sb("ws_rows", [16, 2 * H], U8)
+        ew_win = load_table("ew_win", e_words, nc.scalar)
         gal_t = load_list("gal_t", gal)
-        w3_raw = load_weight("w3_raw", w3_words, nc.scalar)
-        ew_win = load_table("ew_win", e_words)
+        nc.sync.dma_start(ws_rows[:, H : 2 * H].bitcast(I32), w3_scales[0].bitcast(I32))
+        nc.sync.dma_start(ws_rows[:, 0:H].bitcast(I32), w2_scales[0].bitcast(I32))
         for q in range(4):
-            load_scale_rows(es_win, e_scales, q, nc.sync if q % 2 else nc.scalar)
+            load_scale_rows(es_win, e_scales, q, nc.sync)
+        xw_win = load_table("xw_win", x_words, nc.sync)
+        w3_raw = load_weight("w3_raw", w3_words, nc.sync)
         for q in range(4):
-            load_scale_rows(w3s_raw, w3_scales, q, nc.scalar)
+            nc.sync.dma_start(ws_raw[32 * q : 32 * q + 4, :].bitcast(I32), ws_rows[4 * q : 4 * q + 4, :].bitcast(I32))
+        load_unit(0, unit2)
         offs_t = load_list("offs_t", offs)
-        for q in range(4):
-            load_scale_rows(xs_win, x_scales, q, nc.scalar if q == 3 else nc.sync)
         cam_t = load_list("cam_t", cam)
-        w2_raw = load_weight("w2_raw", w2_words, nc.sync)
         for q in range(4):
-            load_scale_rows(w2s_raw, w2_scales, q, nc.sync)
-        xw_win = load_table("xw_win", x_words)
+            load_scale_rows(xs_win, x_scales, q, nc.sync)
+        w2_raw = load_weight("w2_raw", w2_words, nc.sync)
+        load_unit(P, unit)
         w1_raw = load_weight("w1_raw", w1_words, nc.sync)
         for q in range(4):
             load_scale_rows(w1s_raw, w1_scales, q, nc.sync)
@@ -118,15 +126,20 @@ def tile_picked_yreidr_mul_po_kernel(
         nc.vector.tensor_copy(es[:], es_win[:].indirect(gal_t[:]))
         ew = sb("ew", [P, S], U32)
         nc.vector.tensor_copy(ew[:], ew_win[:].bitcast(U32).indirect(gal_t[:]))
-        w3 = deal("w3", w3_raw[:], 2 * H)
-        w3s = deal("w3s", w3s_raw, H)
+        w3 = deal("w3", w3_raw[:], 2 * H, tag="ew_win")
+        w23s = sb("w23s", [P, 2 * H], U8, tag="w3_raw")
+        nc.vector.tensor_copy(
+            w23s[:].bitcast(I32).rearrange("p (w s b q) -> p w s b q", w=2, s=PACK, b=16),
+            ws_raw[:].bitcast(I32).rearrange("p (w b s q) -> p w s b q", w=2, s=PACK, b=16),
+        )
+        w2s, w3s = w23s[:, 0:H], w23s[:, H : 2 * H]
 
-        unit_ps = bank(4, [P, P])
-        nc.tensor.transpose(unit_ps[:], unit_rows[:], ident[:])
-        units = sb("units", [P, 2 * PACK], F32)
-        nc.scalar.copy(units[:], unit_ps[:, 0 : 2 * PACK])
+        unit2_ps = bank(7, [P, P])
+        nc.tensor.transpose(unit2_ps[:], unit_rows[:, 0:P], ident[:])
         unit2_half = sb("unit2_half", [P, PACK], F32)
-        nc.scalar.activation(unit2_half[:], unit_ps[:, PACK : 2 * PACK], ACT.Copy, scale=0.5)
+        nc.scalar.activation(unit2_half[:], unit2_ps[:, 0:PACK], ACT.Copy, scale=0.5)
+        unit2_t = sb("unit2_t", [P, PACK], F32)
+        nc.scalar.copy(unit2_t[:], unit2_ps[:, 0:PACK])
 
         def weight_mm(out, w, ws, s, rhs, rhs_scale):
             nc.tensor.matmul_mx(
@@ -145,46 +158,53 @@ def tile_picked_yreidr_mul_po_kernel(
             weight_mm(b[:], w3, w3s, s, ew[:], es[:])
             yg_ps.append(b)
 
-        xs = sb("xs", [P, S], U8)
-        nc.vector.tensor_copy(xs[:], xs_win[:].indirect(offs_t[:]))
 
-        gcs = []
-        for s in range(PACK):
-            win = sb("yg_win%d" % s, [P, S], F32)
-            gc = sb("gc%d" % s, [P, S], F32)
-            if s == 1:
-                nc.vector.tensor_scalar(win[:], yg_ps[s][:], unit2_half[:, s : s + 1], None, ALU.mult)
-                for h in range(2):
-                    nc.vector.tensor_copy(gc[:, cols(h)], win[:].indirect(half_list(cam_t, h)))
+        xw = sb("xw", [P, S], U32)
+        nc.vector.tensor_copy(xw[:], xw_win[:].bitcast(U32).indirect(offs_t[:]))
+        wins = [sb("yg_win%d" % s, [P, S], F32, tag="xw_win" if s == 1 else None) for s in range(PACK)]
+        gcs = {}
+
+        def cam_gather(s, h):
+            picked = wins[s][:].indirect(half_list(cam_t, h))
+            if (s, h) in ON_VECTOR:
+                gcs[s, h] = sb("gc%d%d" % (s, h), [P, HALF], F32, tag="w1s_raw" if h == 0 else None)
+                nc.vector.tensor_copy(gcs[s, h][:], picked)
             else:
-                nc.scalar.activation(win[:], yg_ps[s][:], ACT.Copy, scale=unit2_half[:, s : s + 1])
-                for h in range(2):
-                    nc.scalar.activation(gc[:, cols(h)], win[:].indirect(half_list(cam_t, h)), ACT.Copy)
-            gcs.append(gc)
+                gcs[s, h] = sb("gc%d%d" % (s, h), [P, HALF], F32)
+                nc.scalar.activation(gcs[s, h][:], picked, ACT.Copy)
+
+        def window(s):
+            if s == 1:
+                nc.vector.tensor_scalar(wins[s][:], yg_ps[s][:], unit2_half[:, s : s + 1], None, ALU.mult)
+            else:
+                nc.scalar.activation(wins[s][:], yg_ps[s][:], ACT.Copy, scale=unit2_half[:, s : s + 1])
+
+        window(0)
+        window(1)
+        window(2)
+        cam_gather(0, 0)
+        window(3)
+        unit_ps = bank(7, [P, P])
+        nc.tensor.transpose(unit_ps[:], unit_rows[:, P : 2 * P], ident[:])
+        unit_t = sb("unit_t", [P, PACK], F32)
+        nc.scalar.copy(unit_t[:], unit_ps[:, 0:PACK])
+        for s in range(1, PACK):
+            if (s, 0) not in ON_VECTOR:
+                cam_gather(s, 0)
+        for s in range(PACK):
+            if (s, 1) not in ON_VECTOR:
+                cam_gather(s, 1)
 
         w2 = deal("w2", w2_raw[:], 2 * H)
-        w2s = deal("w2s", w2s_raw, H)
         ye_ps = []
         for s in range(PACK):
             b = bank(4 + s, [P, S])
             weight_mm(b[:], w2, w2s, s, ew[:], es[:])
             ye_ps.append(b)
-
-        hid2_rows = sb("hid2_rows", [P, PACK, S], BF16)
-
-        def combine(s):
-            nc.vector.scalar_tensor_tensor(
-                hid2_rows[:, s, :], ye_ps[s][:], units[:, PACK + s : PACK + s + 1], gcs[s][:], ALU.mult, ALU.add
-            )
-
-        combine(0)
-        combine(1)
-        xw = sb("xw", [P, S], U32)
-        nc.vector.tensor_copy(xw[:], xw_win[:].bitcast(U32).indirect(offs_t[:]))
-        w1 = deal("w1", w1_raw[:], 2 * H)
-        w1s = deal("w1s", w1s_raw, H)
-        combine(2)
-        combine(3)
+        xs = sb("xs", [P, S], U8)
+        nc.vector.tensor_copy(xs[:], xs_win[:].indirect(offs_t[:]))
+        w1 = deal("w1", w1_raw[:], 2 * H, tag="xs_win")
+        w1s = deal("w1s", w1s_raw[:], H, tag="w1_raw")
 
         pb = sb("pb", [P, PACK, P, PACK], F32)
         for c in range(4):
@@ -195,26 +215,36 @@ def tile_picked_yreidr_mul_po_kernel(
                 pb[:, :, 32 * c : 32 * (c + 1), :], b[:].rearrange("p s (m j) -> p j m s", j=PACK), ACT.Tanh
             )
 
-        hid2_in = sb("hid2_in", [P, S, PACK], BF16)
-        nc.vector.tensor_copy(
-            hid2_in[:].rearrange("p (c i) s -> p c s i", i=4), hid2_rows[:].rearrange("p s (c i) -> p c s i", i=4)
-        )
         hid2_codes = sb("hid2_codes", [P, S], U32)
         hid2_scales = sb("hid2_scales", [P, S], U8)
-        nc.vector.quantize_mx(
-            out=hid2_codes[:].bitcast(FP8X4), scales=hid2_scales[:], in_=hid2_in[:].rearrange("p c s -> p (c s)")
-        )
+        for h in range(2):
+            hid2_rows = sb("hid2_rows%d" % h, [P, PACK, HALF], BF16, tag="gc30" if h else None)
+            for s in range(PACK):
+                if (s + 1, h) in ON_VECTOR:
+                    cam_gather(s + 1, h)
+                nc.vector.scalar_tensor_tensor(
+                    hid2_rows[:, s, :], ye_ps[s][:, cols(h)], unit2_t[:, s : s + 1], gcs[s, h][:], ALU.mult, ALU.add
+                )
+            hid2_in = sb("hid2_in%d" % h, [P, HALF, PACK], BF16)
+            (nc.scalar.copy if h and ILB else nc.vector.tensor_copy)(
+                hid2_in[:].rearrange("p (c i) s -> p c s i", i=4), hid2_rows[:].rearrange("p s (c i) -> p c s i", i=4)
+            )
+            nc.vector.quantize_mx(
+                out=hid2_codes[:, cols(h)].bitcast(FP8X4), scales=hid2_scales[:, cols(h)],
+                in_=hid2_in[:].rearrange("p c s -> p (c s)"),
+            )
 
         sc_ps = []
+        hid_all = sb("hid_in", [P, PACK, P, PACK], BF16, tag="gc31" if ILB else "gc30")
         for j in range(PACK):
-            hid_in = sb("hid_in%d" % j, [P, P, PACK], BF16)
+            hid_in = hid_all[:, j, :, :]
             nc.vector.tensor_tensor(
-                hid_in[:], pb[:, j, :, :], units[:, 0:PACK].unsqueeze(1).to_broadcast([P, P, PACK]), ALU.mult
+                hid_in, pb[:, j, :, :], unit_t[:].unsqueeze(1).to_broadcast([P, P, PACK]), ALU.mult
             )
             hid_codes = sb("hid_codes%d" % j, [P, P], U32)
             hid_scales = sb("hid_scales%d" % j, [P, P], U8)
             nc.vector.quantize_mx(
-                out=hid_codes[:].bitcast(FP8X4), scales=hid_scales[:], in_=hid_in[:].rearrange("p c s -> p (c s)")
+                out=hid_codes[:].bitcast(FP8X4), scales=hid_scales[:], in_=hid_in.rearrange("p c s -> p (c s)")
             )
             b = bank(4 + j, [P, S])
             nc.tensor.matmul_mx(
@@ -223,36 +253,62 @@ def tile_picked_yreidr_mul_po_kernel(
             )
             sc_ps.append(b)
 
+        def ocols(h):
+            return slice(0, SPLIT) if h == 0 else slice(SPLIT, S)
+
+        def olist(lst, h):
+            return lst[:, 0 : SPLIT // 16] if h == 0 else lst[:, SPLIT // 16 : LIST_COLS]
+
+        widths = [SPLIT, S - SPLIT]
         out_rows = out_0.rearrange("(p j) e -> p j e", j=PACK)
         words_out = out_1[0].rearrange("p n t -> p (n t)").bitcast(I32)
         out_codes = sb("out_codes", [P, S], I32)
         out_scales = sb("out_scales", [P, S], U8)
-        sc_win = []
-        for h in range(2):
-            res = sb("res%d" % h, [P, PACK, HALF], F32)
-            for j in range(PACK):
-                if h == 0:
-                    win = sb("sc_win%d" % j, [P, S], F32)
-                    nc.scalar.activation(win[:], sc_ps[j][:], ACT.Copy, bias=-0.15)
-                    sc_win.append(win)
-                s1 = sb("s1_%d_%d" % (h, j), [P, HALF], F32)
-                nc.scalar.activation(s1[:], sc_win[j][:].indirect(half_list(nn1_t, h)), ACT.Copy)
-                ngb = sb("ngb_%d_%d" % (h, j), [P, HALF], F32)
-                nc.vector.tensor_tensor(ngb[:], sc_win[j][:].indirect(half_list(nn2_t, h)), s1[:], ALU.add)
-                nc.vector.tensor_tensor(res[:, j, :], sc_ps[j][:, cols(h)], ngb[:], ALU.mult)
-            nc.sync.dma_start(out_rows[:, :, cols(h)], res[:])
-            res_in = sb("res_in%d" % h, [P, HALF, PACK], BF16)
-            src = res[:].rearrange("p s (c i) -> p c s i", i=4)
-            dst = res_in[:].rearrange("p (c i) s -> p c s i", i=4)
-            if h == 0:
-                nc.scalar.copy(dst, src)
-            else:
-                nc.vector.tensor_copy(dst, src)
+        sc_win = {}
+        s1 = {}
+        steps = STEPS
+        for h, j in steps:
+            if j not in sc_win:
+                sc_win[j] = sb("sc_win%d" % j, [P, S], F32)
+                if j in EV:
+                    nc.vector.tensor_scalar(sc_win[j][:], sc_ps[j][:], -0.15, None, ALU.add)
+                else:
+                    nc.scalar.activation(sc_win[j][:], sc_ps[j][:], ACT.Copy, bias=-0.15)
+            s1[h, j] = sb("s1_%d_%d" % (h, j), [P, widths[h]], F32)
+            nc.scalar.activation(s1[h, j][:], sc_win[j][:].indirect(olist(nn1_t, h)), ACT.Copy)
+
+        res = [sb("res%d" % h, [P, PACK, widths[h]], F32) for h in range(2)]
+        res_in = [sb("res_in%d" % h, [P, widths[h], PACK], BF16) for h in range(2)]
+        ngb = {}
+
+        def neighbours(h, j):
+            ngb[h, j] = sb("ngb_%d_%d" % (h, j), [P, widths[h]], F32)
+            nc.vector.tensor_tensor(ngb[h, j][:], sc_win[j][:].indirect(olist(nn2_t, h)), s1[h, j][:], ALU.add)
+
+        def product(h, j):
+            nc.vector.tensor_tensor(res[h][:, j, :], sc_ps[j][:, ocols(h)], ngb[h, j][:], ALU.mult)
+            if j == PACK - 1:
+                nc.sync.dma_start(out_rows[:, :, ocols(h)], res[h][:])
+
+        def regroup(h, copy):
+            copy(res_in[h][:].rearrange("p (c i) s -> p c s i", i=4), res[h][:].rearrange("p s (c i) -> p c s i", i=4))
+
+        def planes(h):
             nc.vector.quantize_mx(
-                out=out_codes[:, cols(h)].bitcast(FP8X4), scales=out_scales[:, cols(h)],
-                in_=res_in[:].rearrange("p c s -> p (c s)"),
+                out=out_codes[:, ocols(h)].bitcast(FP8X4), scales=out_scales[:, ocols(h)],
+                in_=res_in[h][:].rearrange("p c s -> p (c s)"),
             )
-            nc.sync.dma_start(words_out[:, cols(h)], out_codes[:, cols(h)])
+            nc.sync.dma_start(words_out[:, ocols(h)], out_codes[:, ocols(h)])
+
+        neighbours(*steps[0])
+        for n in range(1, len(steps)):
+            neighbours(*steps[n])
+            product(*steps[n - 1])
+        regroup(0, nc.scalar.copy)
+        product(*steps[-1])
+        planes(0)
+        regroup(1, nc.vector.tensor_copy)
+        planes(1)
         for q in range(4):
             queue = nc.sync if q < 2 else nc.scalar
             queue.dma_start(out_2[0, 4 * q : 4 * q + 4, :].bitcast(I32), out_scales[32 * q : 32 * q + 4, :].bitcast(I32))

@@ -1,6 +1,7 @@
 from contextlib import ExitStack
 
 import concourse.mybir as mybir
+from concourse.masks import make_identity
 
 K, T, S, H = 512, 2048, 512, 512
 FLOPS = 4 * 2 * K * S * H
@@ -18,13 +19,15 @@ ALU = mybir.AluOpType
 
 P = 128
 PACK = 4
+QUADS = 4
+BLOCKS = 16
+RUN = 8
 HALF = S // 2
 LIST_COLS = S // 16
-ON_VECTOR = [(1, 0), (1, 1)]
-SPLIT = 256
-ILB = 1
-EV = []
-STEPS = [(0,0),(1,0),(0,1),(1,1),(0,2),(0,3),(1,2),(1,3)]
+SPARE = 16
+LAST = PACK - 1
+HALVES = [slice(0, HALF), slice(HALF, S)]
+WHOLE = slice(0, S)
 
 
 def tile_picked_yreidr_mul_po_kernel(
@@ -36,8 +39,8 @@ def tile_picked_yreidr_mul_po_kernel(
         keep = ctx.enter_context(tc.tile_pool(name="keep", bufs=1))
         psum = ctx.enter_context(tc.psum_pool(name="psum", bufs=1))
 
-        def sb(name, shape, dtype, tag=None):
-            return keep.tile(shape, dtype, name=name, tag=tag or name, align_bytes=64)
+        def sb(name, shape, dtype, reuse=None):
+            return keep.tile(shape, dtype, name=name, tag=reuse or name, align_bytes=64)
 
         def bank(b, shape):
             return psum.tile(shape, F32, name="bank%d" % b, tag="bank%d" % b)
@@ -47,268 +50,238 @@ def tile_picked_yreidr_mul_po_kernel(
             nc.sync.dma_start(t[:], src)
             return t
 
-        def zeroed_plane(name, width, engine):
+        def offsets(lst, c):
+            return lst[:, c.start // 16 : c.stop // 16]
+
+        def zeroed_plane(name, width):
             t = sb(name, [P, width], U8)
-            engine.memset(t[:].bitcast(I32), 0)
+            nc.vector.memset(t[:].bitcast(I32), 0)
             return t
 
-        def load_scale_rows(t, src, q, queue):
-            queue.dma_start(t[32 * q : 32 * q + 4, :].bitcast(I32), src[0, 4 * q : 4 * q + 4, :].bitcast(I32))
+        def place_scale_rows(plane, rows):
+            for q in range(QUADS):
+                nc.sync.dma_start(plane[32 * q : 32 * q + 4, :].bitcast(I32), rows[4 * q : 4 * q + 4, :].bitcast(I32))
 
         def load_table(name, src, queue):
             t = sb(name, [P, T], I32)
             queue.dma_start(t[:], src[0].rearrange("p n t -> p (n t)").bitcast(I32))
             return t
 
-        def load_weight(name, src, queue):
+        def load_weight(name, src):
             t = sb(name, [P, 2 * H], U8)
-            queue.dma_start(t[:].bitcast(I32), src[0].bitcast(I32))
+            nc.sync.dma_start(t[:].bitcast(I32), src[0].bitcast(I32))
             return t
 
-        def deal(name, raw, width, tag=None):
-            t = sb(name, [P, width], U8, tag=tag)
-            nc.vector.tensor_copy(
-                t[:].bitcast(I32).rearrange("p (s b q) -> p s b q", s=PACK, b=16),
-                raw.bitcast(I32).rearrange("p (b s q) -> p s b q", s=PACK, b=16),
+        def deal_weight(name, raw, engine, reuse=None):
+            t = sb(name, [P, 2 * H], U8, reuse)
+            engine.tensor_copy(
+                t[:].bitcast(I32).rearrange("p (s b q) -> p s b q", s=PACK, b=BLOCKS),
+                raw[:].bitcast(I32).rearrange("p (b s q) -> p s b q", s=PACK, b=BLOCKS),
             )
             return t
 
-        def half_list(lst, h):
-            return lst[:, h * (LIST_COLS // 2) : (h + 1) * (LIST_COLS // 2)]
-
-        def cols(h):
-            return slice(h * HALF, (h + 1) * HALF)
-
-        es_win = zeroed_plane("es_win", T, nc.vector)
-        unit_rows = sb("unit_rows", [P, 2 * P], F32)
-        nc.gpsimd.memset(unit_rows[:], 0.0)
-        ws_raw = zeroed_plane("ws_raw", 2 * H, nc.vector)
-        xs_win = zeroed_plane("xs_win", T, nc.vector)
-        w1s_raw = zeroed_plane("w1s_raw", H, nc.vector)
-        zeros = sb("zeros", [P, P], F32, tag="xw_win")
-        nc.gpsimd.memset(zeros[:], 0.0)
+        es_win = zeroed_plane("es_win", T)
+        ws_raw = zeroed_plane("ws_raw", 3 * H)
+        xs_win = zeroed_plane("xs_win", T)
         ident = sb("ident", [P, P], F32)
-        nc.gpsimd.affine_select(
-            out=ident[:], in_=zeros[:], compare_op=ALU.not_equal, fill=1.0, base=0, pattern=[[-1, P]], channel_multiplier=1
-        )
+        make_identity(nc, ident[:])
+        unit_rows = sb("unit_rows", [P, P], F32)
+        nc.gpsimd.memset(unit_rows[:], 0.0)
 
-        def load_unit(col, src):
-            nc.sync.dma_start(
-                unit_rows[0:PACK, col : col + P].rearrange("s (b r) -> s b r", r=8),
-                src.rearrange("(b s r) o -> s b (r o)", s=PACK, r=8),
+        def load_unit(row, src):
+            nc.gpsimd.dma_start(
+                unit_rows[row : row + PACK, :].rearrange("s (b r) -> s b r", r=RUN),
+                src.rearrange("(b s r) o -> s b (r o)", s=PACK, r=RUN),
             )
 
-        ws_rows = sb("ws_rows", [16, 2 * H], U8)
+        load_unit(PACK, unit2)
+        load_unit(0, unit)
+        ws_rows = sb("ws_rows", [BLOCKS, 3 * H], U8)
         ew_win = load_table("ew_win", e_words, nc.scalar)
         gal_t = load_list("gal_t", gal)
-        nc.sync.dma_start(ws_rows[:, H : 2 * H].bitcast(I32), w3_scales[0].bitcast(I32))
-        nc.sync.dma_start(ws_rows[:, 0:H].bitcast(I32), w2_scales[0].bitcast(I32))
-        for q in range(4):
-            load_scale_rows(es_win, e_scales, q, nc.sync)
-        xw_win = load_table("xw_win", x_words, nc.sync)
-        w3_raw = load_weight("w3_raw", w3_words, nc.sync)
-        for q in range(4):
-            nc.sync.dma_start(ws_raw[32 * q : 32 * q + 4, :].bitcast(I32), ws_rows[4 * q : 4 * q + 4, :].bitcast(I32))
-        load_unit(0, unit2)
+        for n, src in enumerate([w3_scales, w2_scales, w1_scales]):
+            nc.sync.dma_start(ws_rows[:, n * H : (n + 1) * H].bitcast(I32), src[0].bitcast(I32))
+        place_scale_rows(es_win, e_scales[0])
+        w3_raw = load_weight("w3_raw", w3_words)
+        place_scale_rows(ws_raw, ws_rows)
         offs_t = load_list("offs_t", offs)
         cam_t = load_list("cam_t", cam)
-        for q in range(4):
-            load_scale_rows(xs_win, x_scales, q, nc.sync)
-        w2_raw = load_weight("w2_raw", w2_words, nc.sync)
-        load_unit(P, unit)
-        w1_raw = load_weight("w1_raw", w1_words, nc.sync)
-        for q in range(4):
-            load_scale_rows(w1s_raw, w1_scales, q, nc.sync)
+        xw_win = load_table("xw_win", x_words, nc.sync)
+        w2_raw = load_weight("w2_raw", w2_words)
+        place_scale_rows(xs_win, x_scales[0])
+        w1_raw = load_weight("w1_raw", w1_words)
         nn1_t = load_list("nn1_t", nn1)
         nn2_t = load_list("nn2_t", nn2)
+
+        unit_ps = bank(PACK + LAST, [P, P])
+        nc.tensor.transpose(unit_ps[:], unit_rows[:], ident[:])
+        unit2_half = sb("unit2_half", [P, PACK], F32)
+        nc.scalar.activation(unit2_half[:], unit_ps[:, PACK : 2 * PACK], ACT.Copy, scale=0.5)
+        units = sb("units", [P, 2 * PACK], F32)
+        nc.scalar.copy(units[:], unit_ps[:, 0 : 2 * PACK])
 
         es = sb("es", [P, S], U8)
         nc.vector.tensor_copy(es[:], es_win[:].indirect(gal_t[:]))
         ew = sb("ew", [P, S], U32)
         nc.vector.tensor_copy(ew[:], ew_win[:].bitcast(U32).indirect(gal_t[:]))
-        w3 = deal("w3", w3_raw[:], 2 * H, tag="ew_win")
-        w23s = sb("w23s", [P, 2 * H], U8, tag="w3_raw")
+        w3 = deal_weight("w3", w3_raw, nc.vector, reuse="ew_win")
+        ws = sb("ws", [P, 3 * H], U8, reuse="unit_rows")
         nc.vector.tensor_copy(
-            w23s[:].bitcast(I32).rearrange("p (w s b q) -> p w s b q", w=2, s=PACK, b=16),
-            ws_raw[:].bitcast(I32).rearrange("p (w b s q) -> p w s b q", w=2, s=PACK, b=16),
+            ws[:].bitcast(I32).rearrange("p (w s b q) -> p w s b q", w=3, s=PACK, b=BLOCKS),
+            ws_raw[:].bitcast(I32).rearrange("p (w b s q) -> p w s b q", w=3, s=PACK, b=BLOCKS),
         )
-        w2s, w3s = w23s[:, 0:H], w23s[:, H : 2 * H]
+        w3s, w2s, w1s = [ws[:, n * H : (n + 1) * H] for n in range(3)]
 
-        unit2_ps = bank(7, [P, P])
-        nc.tensor.transpose(unit2_ps[:], unit_rows[:, 0:P], ident[:])
-        unit2_half = sb("unit2_half", [P, PACK], F32)
-        nc.scalar.activation(unit2_half[:], unit2_ps[:, 0:PACK], ACT.Copy, scale=0.5)
-        unit2_t = sb("unit2_t", [P, PACK], F32)
-        nc.scalar.copy(unit2_t[:], unit2_ps[:, 0:PACK])
-
-        def weight_mm(out, w, ws, s, rhs, rhs_scale):
+        def weight_product(out, w, plane, s, codes, scales):
             nc.tensor.matmul_mx(
                 out=out,
                 lhsT=w[:, s * 2 * P : (s + 1) * 2 * P].bitcast(FP4X4),
-                lhsT_scale=ws[:, s * P : (s + 1) * P],
-                rhs=rhs.bitcast(FP8X4),
-                rhs_scale=rhs_scale,
+                lhsT_scale=plane[:, s * P : (s + 1) * P],
+                rhs=codes.bitcast(FP8X4),
+                rhs_scale=scales,
                 start=True,
                 stop=True,
             )
 
         yg_ps = []
         for s in range(PACK):
-            b = bank(s, [P, S])
-            weight_mm(b[:], w3, w3s, s, ew[:], es[:])
-            yg_ps.append(b)
-
+            yg_ps.append(bank(s, [P, S]))
+            weight_product(yg_ps[s][:], w3, w3s, s, ew[:], es[:])
 
         xw = sb("xw", [P, S], U32)
-        nc.vector.tensor_copy(xw[:], xw_win[:].bitcast(U32).indirect(offs_t[:]))
-        wins = [sb("yg_win%d" % s, [P, S], F32, tag="xw_win" if s == 1 else None) for s in range(PACK)]
-        gcs = {}
+        nc.vector.tensor_copy(xw[:].rearrange("p (j m) -> p m j", j=PACK), xw_win[:].bitcast(U32).indirect(offs_t[:]))
+        xs_list = sb("xs_list", [P, S], U8)
+        nc.vector.tensor_copy(xs_list[:], xs_win[:].indirect(offs_t[:]))
+        xs = sb("xs", [P, S], U8)
+        nc.vector.tensor_copy(xs[:].rearrange("p (j m) -> p j m", j=PACK), xs_list[:].rearrange("p (m j) -> p j m", j=PACK))
 
-        def cam_gather(s, h):
-            picked = wins[s][:].indirect(half_list(cam_t, h))
-            if (s, h) in ON_VECTOR:
-                gcs[s, h] = sb("gc%d%d" % (s, h), [P, HALF], F32, tag="w1s_raw" if h == 0 else None)
-                nc.vector.tensor_copy(gcs[s, h][:], picked)
-            else:
-                gcs[s, h] = sb("gc%d%d" % (s, h), [P, HALF], F32)
-                nc.scalar.activation(gcs[s, h][:], picked, ACT.Copy)
-
-        def window(s):
-            if s == 1:
-                nc.vector.tensor_scalar(wins[s][:], yg_ps[s][:], unit2_half[:, s : s + 1], None, ALU.mult)
-            else:
-                nc.scalar.activation(wins[s][:], yg_ps[s][:], ACT.Copy, scale=unit2_half[:, s : s + 1])
-
-        window(0)
-        window(1)
-        window(2)
-        cam_gather(0, 0)
-        window(3)
-        unit_ps = bank(7, [P, P])
-        nc.tensor.transpose(unit_ps[:], unit_rows[:, P : 2 * P], ident[:])
-        unit_t = sb("unit_t", [P, PACK], F32)
-        nc.scalar.copy(unit_t[:], unit_ps[:, 0:PACK])
-        for s in range(1, PACK):
-            if (s, 0) not in ON_VECTOR:
-                cam_gather(s, 0)
-        for s in range(PACK):
-            if (s, 1) not in ON_VECTOR:
-                cam_gather(s, 1)
-
-        w2 = deal("w2", w2_raw[:], 2 * H)
+        w2 = deal_weight("w2", w2_raw, nc.gpsimd)
+        w1 = deal_weight("w1", w1_raw, nc.gpsimd)
         ye_ps = []
         for s in range(PACK):
-            b = bank(4 + s, [P, S])
-            weight_mm(b[:], w2, w2s, s, ew[:], es[:])
-            ye_ps.append(b)
-        xs = sb("xs", [P, S], U8)
-        nc.vector.tensor_copy(xs[:], xs_win[:].indirect(offs_t[:]))
-        w1 = deal("w1", w1_raw[:], 2 * H, tag="xs_win")
-        w1s = deal("w1s", w1s_raw[:], H, tag="w1_raw")
+            ye_ps.append(bank(PACK + s, [P, S]))
+            weight_product(ye_ps[s][:], w2, w2s, s, ew[:], es[:])
 
-        pb = sb("pb", [P, PACK, P, PACK], F32)
-        for c in range(4):
-            b = bank(c, [P, PACK, P])
+        whole_slots = [1, 2]
+        yg_win = []
+        for s in range(PACK):
+            yg_win.append(sb("yg_win%d" % s, [P, S + SPARE if s in whole_slots else S], F32))
+            if s in whole_slots:
+                nc.gpsimd.memset(yg_win[s][:, S : S + SPARE], 0.0)
+        gc = [sb("gc%d" % s, [P, S], F32) for s in range(PACK)]
+
+        def scalar_window(s):
+            nc.scalar.activation(yg_win[s][:, WHOLE], yg_ps[s][:], ACT.Copy, scale=unit2_half[:, s : s + 1])
+
+        nc.vector.tensor_scalar(yg_win[0][:], yg_ps[0][:], unit2_half[:, 0:1], None, ALU.mult)
+        scalar_window(1)
+        for h, c in enumerate(HALVES):
+            nc.vector.tensor_copy(gc[0][:, c], yg_win[0][:].indirect(offsets(cam_t, c)))
+            scalar_window(2 + h)
+        for s, c in [(s, WHOLE) for s in whole_slots] + [(LAST, c) for c in HALVES]:
+            nc.scalar.activation(gc[s][:, c], yg_win[s][:].indirect(offsets(cam_t, c)), ACT.Copy)
+
+        pb = [sb("pb%d" % j, [P, P, PACK], F32) for j in range(PACK)]
+
+        def bound(j):
+            y_ps = bank(j, [P, PACK, P])
             for s in range(PACK):
-                weight_mm(b[:, s, :], w1, w1s, s, xw[:, c * P : (c + 1) * P], xs[:, c * P : (c + 1) * P])
-            nc.scalar.activation(
-                pb[:, :, 32 * c : 32 * (c + 1), :], b[:].rearrange("p s (m j) -> p j m s", j=PACK), ACT.Tanh
-            )
+                weight_product(y_ps[:, s, :], w1, w1s, s, xw[:, j * P : (j + 1) * P], xs[:, j * P : (j + 1) * P])
+            nc.scalar.activation(pb[j][:], y_ps[:].rearrange("p s m -> p m s"), ACT.Tanh)
 
+        bound(0)
+        bound(1)
+
+        hid2_rows = sb("hid2_rows", [P, PACK, S], BF16, reuse="xs_win")
+        hid2_in = sb("hid2_in", [P, S, PACK], BF16)
         hid2_codes = sb("hid2_codes", [P, S], U32)
         hid2_scales = sb("hid2_scales", [P, S], U8)
-        for h in range(2):
-            hid2_rows = sb("hid2_rows%d" % h, [P, PACK, HALF], BF16, tag="gc30" if h else None)
-            for s in range(PACK):
-                if (s + 1, h) in ON_VECTOR:
-                    cam_gather(s + 1, h)
-                nc.vector.scalar_tensor_tensor(
-                    hid2_rows[:, s, :], ye_ps[s][:, cols(h)], unit2_t[:, s : s + 1], gcs[s, h][:], ALU.mult, ALU.add
-                )
-            hid2_in = sb("hid2_in%d" % h, [P, HALF, PACK], BF16)
-            (nc.scalar.copy if h and ILB else nc.vector.tensor_copy)(
-                hid2_in[:].rearrange("p (c i) s -> p c s i", i=4), hid2_rows[:].rearrange("p s (c i) -> p c s i", i=4)
+
+        def combine(s, c):
+            nc.vector.scalar_tensor_tensor(
+                hid2_rows[:, s, c], ye_ps[s][:, c], units[:, PACK + s : PACK + s + 1], gc[s][:, c], ALU.mult, ALU.add
             )
+
+        def interleave(copy, dst, src, c):
+            copy(
+                dst[:, c, :].rearrange("p (c i) s -> p c s i", i=4),
+                src[:, :, c].rearrange("p s (c i) -> p c s i", i=4),
+            )
+
+        def quantise(codes, scales, src, c):
             nc.vector.quantize_mx(
-                out=hid2_codes[:, cols(h)].bitcast(FP8X4), scales=hid2_scales[:, cols(h)],
-                in_=hid2_in[:].rearrange("p c s -> p (c s)"),
+                out=codes[:, c].bitcast(FP8X4), scales=scales[:, c], in_=src[:, c, :].rearrange("p c s -> p (c s)")
             )
+
+        hid_codes = [sb("hid_codes%d" % j, [P, P], U32) for j in range(PACK)]
+        hid_scales = [sb("hid_scales%d" % j, [P, P], U8) for j in range(PACK)]
+
+        def quantise_hid(j):
+            hid_in = sb("hid_in%d" % j, [P, P, PACK], BF16)
+            nc.vector.tensor_tensor(hid_in[:], pb[j][:], units[:, 0:PACK].unsqueeze(1).to_broadcast([P, P, PACK]), ALU.mult)
+            quantise(hid_codes[j], hid_scales[j], hid_in, slice(0, P))
+
+        for s in range(LAST):
+            combine(s, WHOLE)
+        combine(LAST, HALVES[0])
+        interleave(nc.scalar.copy, hid2_in, hid2_rows, HALVES[0])
+        combine(LAST, HALVES[1])
+        quantise(hid2_codes, hid2_scales, hid2_in, HALVES[0])
+        interleave(nc.vector.tensor_copy, hid2_in, hid2_rows, HALVES[1])
+        quantise_hid(0)
+        quantise(hid2_codes, hid2_scales, hid2_in, HALVES[1])
+        bound(2)
+        bound(3)
 
         sc_ps = []
-        hid_all = sb("hid_in", [P, PACK, P, PACK], BF16, tag="gc31" if ILB else "gc30")
         for j in range(PACK):
-            hid_in = hid_all[:, j, :, :]
-            nc.vector.tensor_tensor(
-                hid_in, pb[:, j, :, :], unit_t[:].unsqueeze(1).to_broadcast([P, P, PACK]), ALU.mult
-            )
-            hid_codes = sb("hid_codes%d" % j, [P, P], U32)
-            hid_scales = sb("hid_scales%d" % j, [P, P], U8)
-            nc.vector.quantize_mx(
-                out=hid_codes[:].bitcast(FP8X4), scales=hid_scales[:], in_=hid_in.rearrange("p c s -> p (c s)")
-            )
-            b = bank(4 + j, [P, S])
+            if j > 0:
+                quantise_hid(j)
+            sc_ps.append(bank(PACK + j, [P, S]))
             nc.tensor.matmul_mx(
-                out=b[:], lhsT=hid_codes[:].bitcast(FP8X4), lhsT_scale=hid_scales[:],
+                out=sc_ps[j][:], lhsT=hid_codes[j][:].bitcast(FP8X4), lhsT_scale=hid_scales[j][:],
                 rhs=hid2_codes[:].bitcast(FP8X4), rhs_scale=hid2_scales[:], start=True, stop=True,
             )
-            sc_ps.append(b)
 
-        def ocols(h):
-            return slice(0, SPLIT) if h == 0 else slice(SPLIT, S)
+        steps = [(j, h) for j in range(PACK) for h in range(2)]
+        sc_win = [sb("sc_win%d" % j, [P, S], F32) for j in range(PACK)]
+        s1 = [sb("s1_%d" % j, [P, S], F32) for j in range(PACK)]
+        ngb = [sb("ngb_%d" % j, [P, S], F32) for j in range(PACK)]
+        for j, h in steps:
+            if h == 0:
+                nc.scalar.activation(sc_win[j][:], sc_ps[j][:], ACT.Copy, bias=-0.15)
+            nc.scalar.activation(s1[j][:, HALVES[h]], sc_win[j][:].indirect(offsets(nn1_t, HALVES[h])), ACT.Copy)
 
-        def olist(lst, h):
-            return lst[:, 0 : SPLIT // 16] if h == 0 else lst[:, SPLIT // 16 : LIST_COLS]
-
-        widths = [SPLIT, S - SPLIT]
         out_rows = out_0.rearrange("(p j) e -> p j e", j=PACK)
         words_out = out_1[0].rearrange("p n t -> p (n t)").bitcast(I32)
+        res = sb("res", [P, PACK, S], F32)
+        res_in = sb("res_in", [P, S, PACK], BF16)
         out_codes = sb("out_codes", [P, S], I32)
         out_scales = sb("out_scales", [P, S], U8)
-        sc_win = {}
-        s1 = {}
-        steps = STEPS
-        for h, j in steps:
-            if j not in sc_win:
-                sc_win[j] = sb("sc_win%d" % j, [P, S], F32)
-                if j in EV:
-                    nc.vector.tensor_scalar(sc_win[j][:], sc_ps[j][:], -0.15, None, ALU.add)
-                else:
-                    nc.scalar.activation(sc_win[j][:], sc_ps[j][:], ACT.Copy, bias=-0.15)
-            s1[h, j] = sb("s1_%d_%d" % (h, j), [P, widths[h]], F32)
-            nc.scalar.activation(s1[h, j][:], sc_win[j][:].indirect(olist(nn1_t, h)), ACT.Copy)
 
-        res = [sb("res%d" % h, [P, PACK, widths[h]], F32) for h in range(2)]
-        res_in = [sb("res_in%d" % h, [P, widths[h], PACK], BF16) for h in range(2)]
-        ngb = {}
+        def neighbours(j, h):
+            c = HALVES[h]
+            nc.vector.tensor_tensor(ngb[j][:, c], sc_win[j][:].indirect(offsets(nn2_t, c)), s1[j][:, c], ALU.add)
 
-        def neighbours(h, j):
-            ngb[h, j] = sb("ngb_%d_%d" % (h, j), [P, widths[h]], F32)
-            nc.vector.tensor_tensor(ngb[h, j][:], sc_win[j][:].indirect(olist(nn2_t, h)), s1[h, j][:], ALU.add)
+        def product(j, h):
+            c = HALVES[h]
+            nc.vector.tensor_tensor(res[:, j, c], sc_ps[j][:, c], ngb[j][:, c], ALU.mult)
+            if h == 1:
+                nc.sync.dma_start(out_rows[:, j, :], res[:, j, :])
 
-        def product(h, j):
-            nc.vector.tensor_tensor(res[h][:, j, :], sc_ps[j][:, ocols(h)], ngb[h, j][:], ALU.mult)
-            if j == PACK - 1:
-                nc.sync.dma_start(out_rows[:, :, ocols(h)], res[h][:])
-
-        def regroup(h, copy):
-            copy(res_in[h][:].rearrange("p (c i) s -> p c s i", i=4), res[h][:].rearrange("p s (c i) -> p c s i", i=4))
-
-        def planes(h):
-            nc.vector.quantize_mx(
-                out=out_codes[:, ocols(h)].bitcast(FP8X4), scales=out_scales[:, ocols(h)],
-                in_=res_in[h][:].rearrange("p c s -> p (c s)"),
-            )
-            nc.sync.dma_start(words_out[:, ocols(h)], out_codes[:, ocols(h)])
+        def store_words(h):
+            quantise(out_codes, out_scales, res_in, HALVES[h])
+            nc.sync.dma_start(words_out[:, HALVES[h]], out_codes[:, HALVES[h]])
 
         neighbours(*steps[0])
         for n in range(1, len(steps)):
             neighbours(*steps[n])
             product(*steps[n - 1])
-        regroup(0, nc.scalar.copy)
+        interleave(nc.scalar.copy, res_in, res, HALVES[0])
         product(*steps[-1])
-        planes(0)
-        regroup(1, nc.vector.tensor_copy)
-        planes(1)
-        for q in range(4):
-            queue = nc.sync if q < 2 else nc.scalar
+        interleave(nc.vector.tensor_copy, res_in, res, HALVES[1])
+        store_words(1)
+        store_words(0)
+        for q in range(QUADS):
+            queue = nc.sync if q < QUADS // 2 else nc.scalar
             queue.dma_start(out_2[0, 4 * q : 4 * q + 4, :].bitcast(I32), out_scales[32 * q : 32 * q + 4, :].bitcast(I32))

@@ -62,9 +62,9 @@ def tile_picked_yreidr_mul_po_kernel(
             for q in range(QUADS):
                 nc.sync.dma_start(plane[32 * q : 32 * q + 4, :].bitcast(I32), rows[4 * q : 4 * q + 4, :].bitcast(I32))
 
-        def load_table(name, src, queue):
+        def load_table(name, src):
             t = sb(name, [P, T], I32)
-            queue.dma_start(t[:], src[0].rearrange("p n t -> p (n t)").bitcast(I32))
+            nc.sync.dma_start(t[:], src[0].rearrange("p n t -> p (n t)").bitcast(I32))
             return t
 
         def load_weight(name, src):
@@ -81,8 +81,9 @@ def tile_picked_yreidr_mul_po_kernel(
             return t
 
         es_win = zeroed_plane("es_win", T)
-        ws_raw = zeroed_plane("ws_raw", 3 * H)
+        ws_raw = zeroed_plane("ws_raw", 2 * H)
         xs_win = zeroed_plane("xs_win", T)
+        w1s_raw = zeroed_plane("w1s_raw", H)
         ident = sb("ident", [P, P], F32)
         make_identity(nc, ident[:])
         unit_rows = sb("unit_rows", [P, P], F32)
@@ -96,20 +97,21 @@ def tile_picked_yreidr_mul_po_kernel(
 
         load_unit(PACK, unit2)
         load_unit(0, unit)
-        ws_rows = sb("ws_rows", [BLOCKS, 3 * H], U8)
-        ew_win = load_table("ew_win", e_words, nc.scalar)
+        ws_rows = sb("ws_rows", [BLOCKS, 2 * H], U8)
         gal_t = load_list("gal_t", gal)
-        for n, src in enumerate([w3_scales, w2_scales, w1_scales]):
+        ew_win = load_table("ew_win", e_words)
+        for n, src in enumerate([w3_scales, w2_scales]):
             nc.sync.dma_start(ws_rows[:, n * H : (n + 1) * H].bitcast(I32), src[0].bitcast(I32))
         place_scale_rows(es_win, e_scales[0])
+        xw_win = load_table("xw_win", x_words)
         w3_raw = load_weight("w3_raw", w3_words)
         place_scale_rows(ws_raw, ws_rows)
         offs_t = load_list("offs_t", offs)
         cam_t = load_list("cam_t", cam)
-        xw_win = load_table("xw_win", x_words, nc.sync)
         w2_raw = load_weight("w2_raw", w2_words)
         place_scale_rows(xs_win, x_scales[0])
         w1_raw = load_weight("w1_raw", w1_words)
+        place_scale_rows(w1s_raw, w1_scales[0])
         nn1_t = load_list("nn1_t", nn1)
         nn2_t = load_list("nn2_t", nn2)
 
@@ -125,12 +127,12 @@ def tile_picked_yreidr_mul_po_kernel(
         ew = sb("ew", [P, S], U32)
         nc.vector.tensor_copy(ew[:], ew_win[:].bitcast(U32).indirect(gal_t[:]))
         w3 = deal_weight("w3", w3_raw, nc.vector, reuse="ew_win")
-        ws = sb("ws", [P, 3 * H], U8, reuse="unit_rows")
+        ws = sb("ws", [P, 2 * H], U8, reuse="unit_rows")
         nc.vector.tensor_copy(
-            ws[:].bitcast(I32).rearrange("p (w s b q) -> p w s b q", w=3, s=PACK, b=BLOCKS),
-            ws_raw[:].bitcast(I32).rearrange("p (w b s q) -> p w s b q", w=3, s=PACK, b=BLOCKS),
+            ws[:].bitcast(I32).rearrange("p (w s b q) -> p w s b q", w=2, s=PACK, b=BLOCKS),
+            ws_raw[:].bitcast(I32).rearrange("p (w b s q) -> p w s b q", w=2, s=PACK, b=BLOCKS),
         )
-        w3s, w2s, w1s = [ws[:, n * H : (n + 1) * H] for n in range(3)]
+        w3s, w2s = ws[:, 0:H], ws[:, H : 2 * H]
 
         def weight_product(out, w, plane, s, codes, scales):
             nc.tensor.matmul_mx(
@@ -157,6 +159,11 @@ def tile_picked_yreidr_mul_po_kernel(
 
         w2 = deal_weight("w2", w2_raw, nc.gpsimd)
         w1 = deal_weight("w1", w1_raw, nc.gpsimd)
+        w1s = sb("w1s", [P, H], U8)
+        nc.gpsimd.tensor_copy(
+            w1s[:].bitcast(I32).rearrange("p (s b q) -> p s b q", s=PACK, b=BLOCKS),
+            w1s_raw[:].bitcast(I32).rearrange("p (b s q) -> p s b q", s=PACK, b=BLOCKS),
+        )
         ye_ps = []
         for s in range(PACK):
             ye_ps.append(bank(PACK + s, [P, S]))

@@ -268,7 +268,12 @@ def tile_picked_yreidr_mul_po_kernel(
 
         def neighbours(j, h):
             c = HALVES[h]
-            nc.vector.tensor_tensor(ngb[j][:, c], sc_win[j][:].indirect(offsets(nn2_t, c)), s1[j][:, c], ALU.add)
+            picked = sc_win[j][:].indirect(offsets(nn2_t, c))
+            if (j, h) == steps[-1]:
+                s2 = sb("s2", [P, HALF], F32)
+                nc.scalar.activation(s2[:], picked, ACT.Copy)
+                picked = s2[:]
+            nc.vector.tensor_tensor(ngb[j][:, c], picked, s1[j][:, c], ALU.add)
 
         def product(j, h):
             c = HALVES[h]

from contextlib import ExitStack

import concourse.mybir as mybir
from concourse.masks import make_identity

K, T, S, H = 512, 2048, 512, 512
FLOPS = 4 * 2 * K * S * H

F32 = mybir.dt.float32
BF16 = mybir.dt.bfloat16
I32 = mybir.dt.int32
U32 = mybir.dt.uint32
U16 = mybir.dt.uint16
U8 = mybir.dt.uint8
FP8X4 = mybir.dt.float8_e4m3fn_x4
FP4X4 = mybir.dt.float4_e2m1fn_x4
ACT = mybir.ActivationFunctionType
ALU = mybir.AluOpType

P = 128
PACK = 4
QUADS = 4
BLOCKS = 16
RUN = 8
HALF = S // 2
LIST_COLS = S // 16
SPARE = 16
LAST = PACK - 1
HALVES = [slice(0, HALF), slice(HALF, S)]
WHOLE = slice(0, S)


def tile_picked_yreidr_mul_po_kernel(
    tc, x_words, x_scales, w1_words, w1_scales, e_words, e_scales, w2_words, w2_scales, w3_words, w3_scales,
    unit, unit2, offs, gal, cam, nn1, nn2, out_0, out_1, out_2,
):
    nc = tc.nc
    with ExitStack() as ctx:
        keep = ctx.enter_context(tc.tile_pool(name="keep", bufs=1))
        psum = ctx.enter_context(tc.psum_pool(name="psum", bufs=1))

        def sb(name, shape, dtype, reuse=None):
            return keep.tile(shape, dtype, name=name, tag=reuse or name, align_bytes=64)

        def bank(b, shape):
            return psum.tile(shape, F32, name="bank%d" % b, tag="bank%d" % b)

        def load_list(name, src):
            t = keep.tile([P, LIST_COLS], U16, name=name)
            nc.sync.dma_start(t[:], src)
            return t

        def offsets(lst, c):
            return lst[:, c.start // 16 : c.stop // 16]

        def zeroed_plane(name, width):
            t = sb(name, [P, width], U8)
            nc.vector.memset(t[:].bitcast(I32), 0)
            return t

        def place_scale_rows(plane, rows):
            for q in range(QUADS):
                nc.sync.dma_start(plane[32 * q : 32 * q + 4, :].bitcast(I32), rows[4 * q : 4 * q + 4, :].bitcast(I32))

        def load_table(name, src):
            t = sb(name, [P, T], I32)
            nc.sync.dma_start(t[:], src[0].rearrange("p n t -> p (n t)").bitcast(I32))
            return t

        def load_weight(name, src):
            t = sb(name, [P, 2 * H], U8)
            nc.sync.dma_start(t[:].bitcast(I32), src[0].bitcast(I32))
            return t

        def deal_weight(name, raw, engine, reuse=None):
            t = sb(name, [P, 2 * H], U8, reuse)
            engine.tensor_copy(
                t[:].bitcast(I32).rearrange("p (s b q) -> p s b q", s=PACK, b=BLOCKS),
                raw[:].bitcast(I32).rearrange("p (b s q) -> p s b q", s=PACK, b=BLOCKS),
            )
            return t

        es_win = zeroed_plane("es_win", T)
        ws_raw = zeroed_plane("ws_raw", 2 * H)
        xs_win = zeroed_plane("xs_win", T)
        w1s_raw = zeroed_plane("w1s_raw", H)
        ident = sb("ident", [P, P], F32)
        make_identity(nc, ident[:])
        unit_rows = sb("unit_rows", [P, P], F32)
        nc.gpsimd.memset(unit_rows[:], 0.0)

        def load_unit(row, src):
            nc.gpsimd.dma_start(
                unit_rows[row : row + PACK, :].rearrange("s (b r) -> s b r", r=RUN),
                src.rearrange("(b s r) o -> s b (r o)", s=PACK, r=RUN),
            )

        load_unit(PACK, unit2)
        load_unit(0, unit)
        ws_rows = sb("ws_rows", [BLOCKS, 2 * H], U8)
        gal_t = load_list("gal_t", gal)
        ew_win = load_table("ew_win", e_words)
        for n, src in enumerate([w3_scales, w2_scales]):
            nc.sync.dma_start(ws_rows[:, n * H : (n + 1) * H].bitcast(I32), src[0].bitcast(I32))
        place_scale_rows(es_win, e_scales[0])
        xw_win = load_table("xw_win", x_words)
        w3_raw = load_weight("w3_raw", w3_words)
        place_scale_rows(ws_raw, ws_rows)
        offs_t = load_list("offs_t", offs)
        cam_t = load_list("cam_t", cam)
        w2_raw = load_weight("w2_raw", w2_words)
        place_scale_rows(xs_win, x_scales[0])
        w1_raw = load_weight("w1_raw", w1_words)
        place_scale_rows(w1s_raw, w1_scales[0])
        nn1_t = load_list("nn1_t", nn1)
        nn2_t = load_list("nn2_t", nn2)

        unit_ps = bank(PACK + LAST, [P, P])
        nc.tensor.transpose(unit_ps[:], unit_rows[:], ident[:])
        unit2_half = sb("unit2_half", [P, PACK], F32)
        nc.scalar.activation(unit2_half[:], unit_ps[:, PACK : 2 * PACK], ACT.Copy, scale=0.5)
        units = sb("units", [P, 2 * PACK], F32)
        nc.scalar.copy(units[:], unit_ps[:, 0 : 2 * PACK])

        es = sb("es", [P, S], U8)
        nc.vector.tensor_copy(es[:], es_win[:].indirect(gal_t[:]))
        ew = sb("ew", [P, S], U32)
        nc.vector.tensor_copy(ew[:], ew_win[:].bitcast(U32).indirect(gal_t[:]))
        w3 = deal_weight("w3", w3_raw, nc.vector, reuse="ew_win")
        ws = sb("ws", [P, 2 * H], U8, reuse="unit_rows")
        nc.vector.tensor_copy(
            ws[:].bitcast(I32).rearrange("p (w s b q) -> p w s b q", w=2, s=PACK, b=BLOCKS),
            ws_raw[:].bitcast(I32).rearrange("p (w b s q) -> p w s b q", w=2, s=PACK, b=BLOCKS),
        )
        w3s, w2s = ws[:, 0:H], ws[:, H : 2 * H]

        def weight_product(out, w, plane, s, codes, scales):
            nc.tensor.matmul_mx(
                out=out,
                lhsT=w[:, s * 2 * P : (s + 1) * 2 * P].bitcast(FP4X4),
                lhsT_scale=plane[:, s * P : (s + 1) * P],
                rhs=codes.bitcast(FP8X4),
                rhs_scale=scales,
                start=True,
                stop=True,
            )

        yg_ps = []
        for s in range(PACK):
            yg_ps.append(bank(s, [P, S]))
            weight_product(yg_ps[s][:], w3, w3s, s, ew[:], es[:])

        xw = sb("xw", [P, S], U32)
        nc.vector.tensor_copy(xw[:].rearrange("p (j m) -> p m j", j=PACK), xw_win[:].bitcast(U32).indirect(offs_t[:]))
        xs_list = sb("xs_list", [P, S], U8)
        nc.vector.tensor_copy(xs_list[:], xs_win[:].indirect(offs_t[:]))
        xs = sb("xs", [P, S], U8)
        nc.vector.tensor_copy(xs[:].rearrange("p (j m) -> p j m", j=PACK), xs_list[:].rearrange("p (m j) -> p j m", j=PACK))

        w2 = deal_weight("w2", w2_raw, nc.gpsimd)
        w1 = deal_weight("w1", w1_raw, nc.gpsimd)
        w1s = sb("w1s", [P, H], U8)
        nc.gpsimd.tensor_copy(
            w1s[:].bitcast(I32).rearrange("p (s b q) -> p s b q", s=PACK, b=BLOCKS),
            w1s_raw[:].bitcast(I32).rearrange("p (b s q) -> p s b q", s=PACK, b=BLOCKS),
        )
        ye_ps = []
        for s in range(PACK):
            ye_ps.append(bank(PACK + s, [P, S]))
            weight_product(ye_ps[s][:], w2, w2s, s, ew[:], es[:])

        whole_slots = [1, 2]
        yg_win = []
        for s in range(PACK):
            yg_win.append(sb("yg_win%d" % s, [P, S + SPARE if s in whole_slots else S], F32))
            if s in whole_slots:
                nc.gpsimd.memset(yg_win[s][:, S : S + SPARE], 0.0)
        gc = [sb("gc%d" % s, [P, S], F32) for s in range(PACK)]

        def scalar_window(s):
            nc.scalar.activation(yg_win[s][:, WHOLE], yg_ps[s][:], ACT.Copy, scale=unit2_half[:, s : s + 1])

        nc.vector.tensor_scalar(yg_win[0][:], yg_ps[0][:], unit2_half[:, 0:1], None, ALU.mult)
        scalar_window(1)
        for h, c in enumerate(HALVES):
            nc.vector.tensor_copy(gc[0][:, c], yg_win[0][:].indirect(offsets(cam_t, c)))
            scalar_window(2 + h)
        for s, c in [(s, WHOLE) for s in whole_slots] + [(LAST, c) for c in HALVES]:
            nc.scalar.activation(gc[s][:, c], yg_win[s][:].indirect(offsets(cam_t, c)), ACT.Copy)

        pb = [sb("pb%d" % j, [P, P, PACK], F32) for j in range(PACK)]

        def bound(j):
            y_ps = bank(j, [P, PACK, P])
            for s in range(PACK):
                weight_product(y_ps[:, s, :], w1, w1s, s, xw[:, j * P : (j + 1) * P], xs[:, j * P : (j + 1) * P])
            nc.scalar.activation(pb[j][:], y_ps[:].rearrange("p s m -> p m s"), ACT.Tanh)

        bound(0)
        bound(1)

        hid2_rows = sb("hid2_rows", [P, PACK, S], BF16, reuse="xs_win")
        hid2_in = sb("hid2_in", [P, S, PACK], BF16)
        hid2_codes = sb("hid2_codes", [P, S], U32)
        hid2_scales = sb("hid2_scales", [P, S], U8)

        def combine(s, c):
            nc.vector.scalar_tensor_tensor(
                hid2_rows[:, s, c], ye_ps[s][:, c], units[:, PACK + s : PACK + s + 1], gc[s][:, c], ALU.mult, ALU.add
            )

        def interleave(copy, dst, src, c):
            copy(
                dst[:, c, :].rearrange("p (c i) s -> p c s i", i=4),
                src[:, :, c].rearrange("p s (c i) -> p c s i", i=4),
            )

        def quantise(codes, scales, src, c):
            nc.vector.quantize_mx(
                out=codes[:, c].bitcast(FP8X4), scales=scales[:, c], in_=src[:, c, :].rearrange("p c s -> p (c s)")
            )

        hid_codes = [sb("hid_codes%d" % j, [P, P], U32) for j in range(PACK)]
        hid_scales = [sb("hid_scales%d" % j, [P, P], U8) for j in range(PACK)]

        def quantise_hid(j):
            hid_in = sb("hid_in%d" % j, [P, P, PACK], BF16)
            nc.vector.tensor_tensor(hid_in[:], pb[j][:], units[:, 0:PACK].unsqueeze(1).to_broadcast([P, P, PACK]), ALU.mult)
            quantise(hid_codes[j], hid_scales[j], hid_in, slice(0, P))

        for s in range(LAST):
            combine(s, WHOLE)
        combine(LAST, HALVES[0])
        interleave(nc.scalar.copy, hid2_in, hid2_rows, HALVES[0])
        combine(LAST, HALVES[1])
        quantise(hid2_codes, hid2_scales, hid2_in, HALVES[0])
        interleave(nc.vector.tensor_copy, hid2_in, hid2_rows, HALVES[1])
        quantise_hid(0)
        quantise(hid2_codes, hid2_scales, hid2_in, HALVES[1])
        bound(2)
        bound(3)

        sc_ps = []
        for j in range(PACK):
            if j > 0:
                quantise_hid(j)
            sc_ps.append(bank(PACK + j, [P, S]))
            nc.tensor.matmul_mx(
                out=sc_ps[j][:], lhsT=hid_codes[j][:].bitcast(FP8X4), lhsT_scale=hid_scales[j][:],
                rhs=hid2_codes[:].bitcast(FP8X4), rhs_scale=hid2_scales[:], start=True, stop=True,
            )

        steps = [(j, h) for j in range(PACK) for h in range(2)]
        sc_win = [sb("sc_win%d" % j, [P, S], F32) for j in range(PACK)]
        s1 = [sb("s1_%d" % j, [P, S], F32) for j in range(PACK)]
        ngb = [sb("ngb_%d" % j, [P, S], F32) for j in range(PACK)]
        for j, h in steps:
            if h == 0:
                nc.scalar.activation(sc_win[j][:], sc_ps[j][:], ACT.Copy, bias=-0.15)
            nc.scalar.activation(s1[j][:, HALVES[h]], sc_win[j][:].indirect(offsets(nn1_t, HALVES[h])), ACT.Copy)

        out_rows = out_0.rearrange("(p j) e -> p j e", j=PACK)
        words_out = out_1[0].rearrange("p n t -> p (n t)").bitcast(I32)
        res = sb("res", [P, PACK, S], F32)
        res_in = sb("res_in", [P, S, PACK], BF16)
        out_codes = sb("out_codes", [P, S], I32)
        out_scales = sb("out_scales", [P, S], U8)

        def neighbours(j, h):
            c = HALVES[h]
            picked = sc_win[j][:].indirect(offsets(nn2_t, c))
            if (j, h) == steps[-1]:
                s2 = sb("s2", [P, HALF], F32)
                nc.scalar.activation(s2[:], picked, ACT.Copy)
                picked = s2[:]
            nc.vector.tensor_tensor(ngb[j][:, c], picked, s1[j][:, c], ALU.add)

        def product(j, h):
            c = HALVES[h]
            nc.vector.tensor_tensor(res[:, j, c], sc_ps[j][:, c], ngb[j][:, c], ALU.mult)
            if h == 1:
                nc.sync.dma_start(out_rows[:, j, :], res[:, j, :])

        def store_words(h):
            quantise(out_codes, out_scales, res_in, HALVES[h])
            nc.sync.dma_start(words_out[:, HALVES[h]], out_codes[:, HALVES[h]])

        neighbours(*steps[0])
        for n in range(1, len(steps)):
            neighbours(*steps[n])
            product(*steps[n - 1])
        interleave(nc.scalar.copy, res_in, res, HALVES[0])
        product(*steps[-1])
        interleave(nc.vector.tensor_copy, res_in, res, HALVES[1])
        store_words(1)
        store_words(0)
        for q in range(QUADS):
            queue = nc.sync if q < QUADS // 2 else nc.scalar
            queue.dma_start(out_2[0, 4 * q : 4 * q + 4, :].bitcast(I32), out_scales[32 * q : 32 * q + 4, :].bitcast(I32))
